import numpy as np
import ml_dtypes


def mxq(x, axis, fmt="e4m3"):
    dtype, down = {"e4m3": (ml_dtypes.float8_e4m3fn, 7), "e5m2": (ml_dtypes.float8_e5m2, 14)}[fmt]
    v = np.moveaxis(np.asarray(x, np.float32).astype(ml_dtypes.bfloat16).astype(np.float64), axis, -1)
    blocks = v.reshape(v.shape[:-1] + (-1, 32))
    amax = np.abs(blocks).max(-1, keepdims=True)
    byte = np.maximum(np.where(amax > 0, np.frexp(amax)[1] - 1 + 127, 0) - down, 1)
    scale = np.exp2(byte - 127.0)
    codes = (blocks / scale).astype(np.float32).astype(dtype).astype(np.float64)
    return np.moveaxis((codes * scale).reshape(v.shape), -1, axis)


WIDE = False


def mx_kscale(k):
    if not WIDE:
        return np.ones(k)
    levels = np.array([10, -10, 5, -5, 0])
    if k % 512:
        return np.exp2(np.random.permutation(np.resize(levels, k // 32))).repeat(32)
    a = np.empty((k // 512, 16))
    for p in range(k // 512):
        a[p, :8] = np.random.permutation(np.resize(levels, 8))
        for g in range(8):
            far = levels[np.abs(levels - a[p, g]) >= 10]
            a[p, g + 8] = far[np.random.randint(len(far))]
    return np.exp2(a.ravel()).repeat(32)


def f64(x):
    return np.asarray(x).astype(np.float64)


def striped8(idx):
    return np.concatenate([x.reshape(-1, 16).T for x in idx]).astype(np.uint16)


def runs(offs, k):
    lists = np.stack([offs[16 * r : 16 * r + 16].T.reshape(-1) for r in range(8)]).astype(np.int64)
    return lists[np.arange(k) % 512 // 64]


def pack_weight(w):
    k, n = w.shape
    w = f64(np.asarray(w, np.float32).astype(ml_dtypes.bfloat16)).reshape(k // 32, 32, n)
    amax = np.abs(w).max(1)
    byte = np.clip(np.where(amax > 0, np.frexp(amax)[1] - 1 + 127 - 7, 1), 1, 254)
    scaled = (w * np.exp2(127.0 - byte)[:, None, :]).reshape(k, n).astype(np.float32)
    words = np.ascontiguousarray(scaled.reshape(k // 512, 128, 4, n).transpose(0, 1, 3, 2)).astype(ml_dtypes.float8_e4m3fn).view(np.uint8)
    return words, np.ascontiguousarray(byte.astype(np.uint8).reshape(k // 512, 16, n))


def unpack_weight(words, scales):
    g, p, n, _ = words.shape
    vals = np.ascontiguousarray(words).view(ml_dtypes.float8_e4m3fn).astype(np.float64) * np.repeat(np.exp2(scales.astype(np.float64) - 127.0), 8, axis=1)[..., None]
    return vals.transpose(0, 1, 3, 2).reshape(g * 512, n)


K, T, S, N, H = 512, 2048, 512, 512, 512


def setup_inputs():
    n = np.random.standard_normal
    s = mx_kscale(K)[:, None]
    u = mx_kscale(H)
    packed_xT = pack_weight(n((K, T)) * s)
    return {
        "x_words": packed_xT[0],
        "x_scales": packed_xT[1],
        "w1": (n((K, H)) / np.sqrt(K) / s).astype(np.float32),
        "gn": (np.random.uniform(0.5, 1.5, (H, 1)) * u[:, None]).astype(np.float32),
        "w2": (n((H, N)) / np.sqrt(H) / u[:, None]).astype(np.float32),
        "offs": striped8(np.random.randint(0, T, (8, S))),
        "n1": striped8(np.stack([np.random.permutation(S) for _ in range(8)])),
        "n2": striped8(np.stack([np.random.permutation(S) for _ in range(8)])),
    }


def reference(x_words, x_scales, w1, gn, w2, offs, n1, n2):
    xq = unpack_weight(x_words, x_scales)[np.arange(K)[:, None], runs(offs, K)]
    y = mxq(f64(w1), 0, "e4m3").T @ xq
    p = (y[np.arange(H)[:, None], runs(n1, H)]) * (y[np.arange(H)[:, None], runs(n2, H)])
    z = f64(gn) * (p[np.arange(H)[:, None], runs(n1, H)] - (0.5 * p))
    return mxq(f64(w2), 0, "e4m3").T @ mxq(z, 0, "e4m3")

@@ -1,0 +1,171 @@
+from contextlib import ExitStack
+
+import concourse.mybir as mybir
+
+K, T, S, N, H = 512, 2048, 512, 512, 512
+FLOPS = 2 * K * H * S + 2 * H * N * S
+
+F32 = mybir.dt.float32
+BF16 = mybir.dt.bfloat16
+I32 = mybir.dt.int32
+U32 = mybir.dt.uint32
+U16 = mybir.dt.uint16
+U8 = mybir.dt.uint8
+FP8X4 = mybir.dt.float8_e4m3fn_x4
+MULT = mybir.AluOpType.mult
+SUB = mybir.AluOpType.subtract
+COPY = mybir.ActivationFunctionType.Copy
+
+P = 128
+PACK = 4
+HALF = S // 2
+W1_SPLIT = 88
+CHUNKS = ((0, 256), (256, 128), (384, 128))
+
+
+def entries(lists, start, count):
+    return lists[:, start // 16 : (start + count) // 16]
+
+
+def tile_picked_hashprod_none_p_kernel(tc, x_words, x_scales, w1, gn, w2, offs, n1, n2, out):
+    nc = tc.nc
+    with ExitStack() as ctx:
+        keep = ctx.enter_context(tc.tile_pool(name="keep", bufs=1))
+        psum = ctx.enter_context(tc.psum_pool(name="psum", bufs=8))
+
+        offs_sb = keep.tile([P, S // 16], U16, name="offs_sb")
+        nc.sync.dma_start(offs_sb[:], offs)
+        scale_table = keep.tile([P, T], U8, name="scale_table")
+        nc.sync.dma_start(
+            scale_table[:].bitcast(I32),
+            x_scales[0].bitcast(I32).unsqueeze(1).broadcast_to([16, 8, T // 4]),
+        )
+        gain = keep.tile([P, PACK], F32, name="gain")
+        nc.sync.dma_start(gain[:], gn.rearrange("(p t) o -> p (t o)", t=PACK))
+        w1_raw = keep.tile([P, PACK * H], F32, name="w1_raw")
+        nc.sync.dma_start(w1_raw[:], w1.rearrange("(p j) c -> p (j c)", j=PACK))
+        word_table = keep.tile([P, T], U32, name="word_table")
+        nc.sync.dma_start(word_table[:].bitcast(I32), x_words[0].rearrange("p c r -> p (c r)").bitcast(I32))
+        n1_sb = keep.tile([P, S // 16], U16, name="n1_sb")
+        nc.sync.dma_start(n1_sb[:], n1)
+        n2_sb = keep.tile([P, S // 16], U16, name="n2_sb")
+        nc.sync.dma_start(n2_sb[:], n2)
+        w2_raw = keep.tile([P, PACK * N], F32, name="w2_raw")
+        nc.sync.dma_start(w2_raw[:], w2.rearrange("(p j) c -> p (j c)", j=PACK))
+        half_gain = keep.tile([P, PACK], F32, name="half_gain")
+        nc.scalar.mul(half_gain[:], gain[:], 0.5)
+
+        picked_bytes = keep.tile([P, S], U8, name="picked_bytes", align_bytes=64)
+        nc.vector.tensor_copy(picked_bytes[:], scale_table[:].indirect(offs_sb[:]))
+        x_plane = keep.tile([P, S], U8, name="x_plane", align_bytes=64)
+        nc.vector.tensor_copy(x_plane[:].bitcast(I32), picked_bytes[:].bitcast(I32))
+        for b in range(1, 4):
+            nc.scalar.dma_start(x_plane[b:P:32, :].bitcast(I32), picked_bytes[8 * b : P : 32, :].bitcast(I32))
+
+        w1_grouped = keep.tile([P, PACK * H], BF16, name="w1_grouped", align_bytes=64)
+        w1_dst = w1_grouped[:].rearrange("p (t m j) -> p m t j", t=PACK, j=PACK)
+        w1_src = w1_raw[:].rearrange("p (j m t) -> p m t j", j=PACK, t=PACK)
+        nc.vector.tensor_copy(w1_dst[:, :W1_SPLIT], w1_src[:, :W1_SPLIT])
+        nc.scalar.copy(w1_dst[:, W1_SPLIT:], w1_src[:, W1_SPLIT:])
+        w1_codes = keep.tile([P, H], U32, name="w1_codes", align_bytes=64)
+        w1_plane = keep.tile([P, H], U8, name="w1_plane", align_bytes=64)
+        nc.vector.quantize_mx(out=w1_codes[:].bitcast(FP8X4), scales=w1_plane[:], in_=w1_grouped[:])
+
+        x_codes = keep.tile([P, S], U32, name="x_codes", align_bytes=64)
+        for c0 in range(0, S, HALF):
+            nc.vector.tensor_copy(x_codes[:, c0 : c0 + HALF], word_table[:].indirect(entries(offs_sb, c0, HALF)))
+
+        y = [keep.tile([P, S], F32, name=f"y{t}") for t in range(PACK)]
+        for t in range(PACK):
+            rows = slice(t * P, (t + 1) * P)
+            width = HALF if t == 0 else S
+            for c0 in range(0, S, width):
+                cols = slice(c0, c0 + width)
+                bank = psum.tile([P, S], F32, name="bank")
+                nc.tensor.matmul_mx(
+                    out=bank[:, :width],
+                    lhsT=w1_codes[:, rows].bitcast(FP8X4),
+                    lhsT_scale=w1_plane[:, rows],
+                    rhs=x_codes[:, cols].bitcast(FP8X4),
+                    rhs_scale=x_plane[:, cols],
+                    start=True,
+                    stop=True,
+                )
+                nc.scalar.copy(y[t][:, cols], bank[:, :width])
+
+        w2_grouped = keep.tile([P, PACK * N], BF16, name="w2_grouped", align_bytes=64)
+        w2_dst = w2_grouped[:].rearrange("p (c i j) -> p c j i", i=4, j=PACK)
+        w2_src = w2_raw[:].rearrange("p (j c i) -> p c j i", i=4, j=PACK)
+        w2_codes = keep.tile([P, N], U32, name="w2_codes", align_bytes=64)
+        w2_plane = keep.tile([P, N], U8, name="w2_plane", align_bytes=64)
+
+        scaled = []
+        halved = []
+        for t in range(PACK):
+            first = keep.tile([P, S], F32, name=f"first{t}")
+            prod = keep.tile([P, S], F32, name=f"prod{t}")
+            for c0 in range(0, S, HALF):
+                nc.vector.tensor_copy(first[:, c0 : c0 + HALF], y[t][:].indirect(entries(n1_sb, c0, HALF)))
+            for c0 in range(0, S, HALF):
+                nc.vector.tensor_tensor(
+                    prod[:, c0 : c0 + HALF], y[t][:].indirect(entries(n2_sb, c0, HALF)), first[:, c0 : c0 + HALF], MULT
+                )
+            nc.scalar.copy(w2_dst[:, 32 * t : 32 * (t + 1)], w2_src[:, 32 * t : 32 * (t + 1)])
+            full = keep.tile([P, S], F32, name=f"scaled{t}")
+            half = keep.tile([P, S], F32, name=f"halved{t}")
+            nc.scalar.activation(full[:], prod[:], COPY, scale=gain[:, t : t + 1])
+            nc.scalar.activation(half[:], prod[:], COPY, scale=half_gain[:, t : t + 1])
+            scaled.append(full)
+            halved.append(half)
+        nc.vector.quantize_mx(out=w2_codes[:].bitcast(FP8X4), scales=w2_plane[:], in_=w2_grouped[:])
+
+        out_rows = out.rearrange("(t p) j -> p t j", p=P)
+
+        def gather_chunk(c0, n):
+            z = keep.tile([P, PACK * n], F32, name=f"z{c0}")
+            for t in range(PACK):
+                nc.vector.tensor_tensor(
+                    z[:, t * n : (t + 1) * n], scaled[t][:].indirect(entries(n1_sb, c0, n)), halved[t][:, c0 : c0 + n], SUB
+                )
+            grouped = keep.tile([P, PACK * n], BF16, name=f"z_grouped{c0}", align_bytes=64)
+            dst = grouped[:].rearrange("p (c i t) -> p c t i", i=4, t=PACK)
+            src = z[:].rearrange("p (t c i) -> p c t i", i=4, t=PACK)
+            if c0 + n == S:
+                nc.vector.tensor_copy(dst, src)
+            else:
+                nc.scalar.copy(dst, src)
+            return grouped
+
+        def finish_chunk(c0, n, grouped):
+            codes = keep.tile([P, n], U32, name=f"z_codes{c0}", align_bytes=64)
+            plane = keep.tile([P, n], U8, name=f"z_plane{c0}", align_bytes=64)
+            nc.vector.quantize_mx(out=codes[:].bitcast(FP8X4), scales=plane[:], in_=grouped[:])
+            for pair in range(2):
+                bank = psum.tile([P, S], F32, name="bank")
+                for u in range(2):
+                    rows = slice((2 * pair + u) * P, (2 * pair + u + 1) * P)
+                    nc.tensor.matmul_mx(
+                        out=bank[:, u * n : (u + 1) * n],
+                        lhsT=w2_codes[:, rows].bitcast(FP8X4),
+                        lhsT_scale=w2_plane[:, rows],
+                        rhs=codes[:].bitcast(FP8X4),
+                        rhs_scale=plane[:],
+                        start=True,
+                        stop=True,
+                    )
+                result = keep.tile([P, 2 * n], F32, name=f"result{c0}_{pair}")
+                if c0 + n == S and pair == 1:
+                    nc.vector.tensor_copy(result[:], bank[:, : 2 * n])
+                else:
+                    nc.scalar.copy(result[:], bank[:, : 2 * n])
+                nc.sync.dma_start(
+                    out_rows[:, 2 * pair : 2 * pair + 2, c0 : c0 + n], result[:].rearrange("p (u j) -> p u j", u=2)
+                )
+
+        pending = None
+        for c0, n in CHUNKS:
+            grouped = gather_chunk(c0, n)
+            if pending is not None:
+                finish_chunk(*pending)
+            pending = (c0, n, grouped)
+        finish_chunk(*pending)

@@ -40,27 +40,23 @@ def tile_picked_hashprod_none_p_kernel(tc, x_words, x_scales, w1, gn, w2, offs, 
             scale_table[:].bitcast(I32),
             x_scales[0].bitcast(I32).unsqueeze(1).broadcast_to([16, 8, T // 4]),
         )
-        gain = keep.tile([P, PACK], F32, name="gain")
-        nc.sync.dma_start(gain[:], gn.rearrange("(p t) o -> p (t o)", t=PACK))
-        w1_raw = keep.tile([P, PACK * H], F32, name="w1_raw")
+        w1_raw = keep.tile([P, PACK * H], F32, name="w1_raw", tag="raw")
         nc.sync.dma_start(w1_raw[:], w1.rearrange("(p j) c -> p (j c)", j=PACK))
         word_table = keep.tile([P, T], U32, name="word_table")
         nc.sync.dma_start(word_table[:].bitcast(I32), x_words[0].rearrange("p c r -> p (c r)").bitcast(I32))
+        gain = keep.tile([P, PACK], F32, name="gain")
+        nc.sync.dma_start(gain[:], gn.rearrange("(p t) o -> p (t o)", t=PACK))
         n1_sb = keep.tile([P, S // 16], U16, name="n1_sb")
         nc.sync.dma_start(n1_sb[:], n1)
         n2_sb = keep.tile([P, S // 16], U16, name="n2_sb")
         nc.sync.dma_start(n2_sb[:], n2)
-        w2_raw = keep.tile([P, PACK * N], F32, name="w2_raw")
-        nc.sync.dma_start(w2_raw[:], w2.rearrange("(p j) c -> p (j c)", j=PACK))
-        half_gain = keep.tile([P, PACK], F32, name="half_gain")
-        nc.scalar.mul(half_gain[:], gain[:], 0.5)
 
         picked_bytes = keep.tile([P, S], U8, name="picked_bytes", align_bytes=64)
         nc.vector.tensor_copy(picked_bytes[:], scale_table[:].indirect(offs_sb[:]))
         x_plane = keep.tile([P, S], U8, name="x_plane", align_bytes=64)
         nc.vector.tensor_copy(x_plane[:].bitcast(I32), picked_bytes[:].bitcast(I32))
         for b in range(1, 4):
-            nc.scalar.dma_start(x_plane[b:P:32, :].bitcast(I32), picked_bytes[8 * b : P : 32, :].bitcast(I32))
+            nc.sync.dma_start(x_plane[b:P:32, :].bitcast(I32), picked_bytes[8 * b : P : 32, :].bitcast(I32))
 
         w1_grouped = keep.tile([P, PACK * H], BF16, name="w1_grouped", align_bytes=64)
         w1_dst = w1_grouped[:].rearrange("p (t m j) -> p m t j", t=PACK, j=PACK)
@@ -71,14 +67,20 @@ def tile_picked_hashprod_none_p_kernel(tc, x_words, x_scales, w1, gn, w2, offs, 
         w1_plane = keep.tile([P, H], U8, name="w1_plane", align_bytes=64)
         nc.vector.quantize_mx(out=w1_codes[:].bitcast(FP8X4), scales=w1_plane[:], in_=w1_grouped[:])
 
+        w2_raw = keep.tile([P, PACK * N], F32, name="w2_raw", tag="raw")
+        nc.sync.dma_start(w2_raw[:], w2.rearrange("(p j) c -> p (j c)", j=PACK))
+
         x_codes = keep.tile([P, S], U32, name="x_codes", align_bytes=64)
         for c0 in range(0, S, HALF):
             nc.vector.tensor_copy(x_codes[:, c0 : c0 + HALF], word_table[:].indirect(entries(offs_sb, c0, HALF)))
 
-        y = [keep.tile([P, S], F32, name=f"y{t}") for t in range(PACK)]
+        y = [keep.tile([P, 2 * S], F32, name=f"y{t}") for t in range(PACK)]
+        gained = [keep.tile([P, 2 * S], F32, name=f"gained{t}") for t in range(PACK)]
+        banks = []
         for t in range(PACK):
             rows = slice(t * P, (t + 1) * P)
             width = HALF if t == 0 else S
+            parts = []
             for c0 in range(0, S, width):
                 cols = slice(c0, c0 + width)
                 bank = psum.tile([P, S], F32, name="bank")
@@ -92,6 +94,13 @@ def tile_picked_hashprod_none_p_kernel(tc, x_words, x_scales, w1, gn, w2, offs, 
                     stop=True,
                 )
                 nc.scalar.copy(y[t][:, cols], bank[:, :width])
+                parts.append((cols, bank[:, :width]))
+            banks.append(parts)
+            if t > 0:
+                for cols, part in banks[t - 1]:
+                    nc.scalar.activation(gained[t - 1][:, cols], part, COPY, scale=gain[:, t - 1 : t])
+        for cols, part in banks[PACK - 1]:
+            nc.scalar.activation(gained[PACK - 1][:, cols], part, COPY, scale=gain[:, PACK - 1 : PACK])
 
         w2_grouped = keep.tile([P, PACK * N], BF16, name="w2_grouped", align_bytes=64)
         w2_dst = w2_grouped[:].rearrange("p (c i j) -> p c j i", i=4, j=PACK)
@@ -99,35 +108,30 @@ def tile_picked_hashprod_none_p_kernel(tc, x_words, x_scales, w1, gn, w2, offs, 
         w2_codes = keep.tile([P, N], U32, name="w2_codes", align_bytes=64)
         w2_plane = keep.tile([P, N], U8, name="w2_plane", align_bytes=64)
 
-        scaled = []
-        halved = []
+        firsts = [keep.tile([P, S], F32, name=f"first{t}") for t in range(PACK)]
+        scaled = [keep.tile([P, S], F32, name=f"scaled{t}") for t in range(PACK)]
+        halved = [keep.tile([P, S], F32, name=f"halved{t}") for t in range(PACK)]
+        nc.vector.tensor_copy(firsts[0][:], y[0][:].indirect(n1_sb[:]))
         for t in range(PACK):
-            first = keep.tile([P, S], F32, name=f"first{t}")
-            prod = keep.tile([P, S], F32, name=f"prod{t}")
-            for c0 in range(0, S, HALF):
-                nc.vector.tensor_copy(first[:, c0 : c0 + HALF], y[t][:].indirect(entries(n1_sb, c0, HALF)))
-            for c0 in range(0, S, HALF):
-                nc.vector.tensor_tensor(
-                    prod[:, c0 : c0 + HALF], y[t][:].indirect(entries(n2_sb, c0, HALF)), first[:, c0 : c0 + HALF], MULT
-                )
+            if t + 1 < PACK:
+                nc.vector.tensor_copy(firsts[t + 1][:], y[t + 1][:].indirect(n1_sb[:]))
+            nc.vector.tensor_tensor(scaled[t][:], gained[t][:].indirect(n2_sb[:]), firsts[t][:], MULT)
             nc.scalar.copy(w2_dst[:, 32 * t : 32 * (t + 1)], w2_src[:, 32 * t : 32 * (t + 1)])
-            full = keep.tile([P, S], F32, name=f"scaled{t}")
-            half = keep.tile([P, S], F32, name=f"halved{t}")
-            nc.scalar.activation(full[:], prod[:], COPY, scale=gain[:, t : t + 1])
-            nc.scalar.activation(half[:], prod[:], COPY, scale=half_gain[:, t : t + 1])
-            scaled.append(full)
-            halved.append(half)
+            nc.scalar.mul(halved[t][:], scaled[t][:], 0.5)
         nc.vector.quantize_mx(out=w2_codes[:].bitcast(FP8X4), scales=w2_plane[:], in_=w2_grouped[:])
 
         out_rows = out.rearrange("(t p) j -> p t j", p=P)
 
         def gather_chunk(c0, n):
-            z = keep.tile([P, PACK * n], F32, name=f"z{c0}")
+            z = keep.tile([P, PACK * n], F32, name=f"z{c0}", tag="turn_a" if c0 + n == S else f"z{c0}", align_bytes=64)
             for t in range(PACK):
                 nc.vector.tensor_tensor(
                     z[:, t * n : (t + 1) * n], scaled[t][:].indirect(entries(n1_sb, c0, n)), halved[t][:, c0 : c0 + n], SUB
                 )
-            grouped = keep.tile([P, PACK * n], BF16, name=f"z_grouped{c0}", align_bytes=64)
+            return z
+
+        def group_chunk(c0, n, z):
+            grouped = keep.tile([P, PACK * n], BF16, name=f"z_grouped{c0}", tag="turn_a" if c0 == 0 else "turn_b", align_bytes=64)
             dst = grouped[:].rearrange("p (c i t) -> p c t i", i=4, t=PACK)
             src = z[:].rearrange("p (t c i) -> p c t i", i=4, t=PACK)
             if c0 + n == S:
@@ -158,14 +162,15 @@ def tile_picked_hashprod_none_p_kernel(tc, x_words, x_scales, w1, gn, w2, offs, 
                     nc.vector.tensor_copy(result[:], bank[:, : 2 * n])
                 else:
                     nc.scalar.copy(result[:], bank[:, : 2 * n])
-                nc.sync.dma_start(
+                queue = nc.scalar if c0 + n == S and pair == 0 else nc.sync
+                queue.dma_start(
                     out_rows[:, 2 * pair : 2 * pair + 2, c0 : c0 + n], result[:].rearrange("p (u j) -> p u j", u=2)
                 )
 
-        pending = None
-        for c0, n in CHUNKS:
-            grouped = gather_chunk(c0, n)
-            if pending is not None:
-                finish_chunk(*pending)
-            pending = (c0, n, grouped)
-        finish_chunk(*pending)
+        first_chunk, second_chunk, last_chunk = CHUNKS
+        grouped_first = group_chunk(*first_chunk, gather_chunk(*first_chunk))
+        grouped_second = group_chunk(*second_chunk, gather_chunk(*second_chunk))
+        finish_chunk(*first_chunk, grouped_first)
+        z_last = gather_chunk(*last_chunk)
+        finish_chunk(*second_chunk, grouped_second)
+        finish_chunk(*last_chunk, group_chunk(*last_chunk, z_last))

@@ -19,7 +19,7 @@ COPY = mybir.ActivationFunctionType.Copy
 P = 128
 PACK = 4
 HALF = S // 2
-W1_SPLIT = 88
+W1_EARLY = 256
 CHUNKS = ((0, 256), (256, 128), (384, 128))
 
 
@@ -40,10 +40,13 @@ def tile_picked_hashprod_none_p_kernel(tc, x_words, x_scales, w1, gn, w2, offs, 
             scale_table[:].bitcast(I32),
             x_scales[0].bitcast(I32).unsqueeze(1).broadcast_to([16, 8, T // 4]),
         )
-        w1_raw = keep.tile([P, PACK * H], F32, name="w1_raw", tag="raw")
-        nc.sync.dma_start(w1_raw[:], w1.rearrange("(p j) c -> p (j c)", j=PACK))
         word_table = keep.tile([P, T], U32, name="word_table")
         nc.sync.dma_start(word_table[:].bitcast(I32), x_words[0].rearrange("p c r -> p (c r)").bitcast(I32))
+        w1_rows = w1.rearrange("(p j) c -> p j c", j=PACK)
+        w1_early = keep.tile([P, PACK * W1_EARLY], F32, name="w1_early", tag="raw")
+        nc.sync.dma_start(w1_early[:].rearrange("p (j c) -> p j c", j=PACK), w1_rows[:, :, :W1_EARLY])
+        w1_late = keep.tile([P, PACK * (H - W1_EARLY)], F32, name="w1_late")
+        nc.sync.dma_start(w1_late[:].rearrange("p (j c) -> p j c", j=PACK), w1_rows[:, :, W1_EARLY:])
         gain = keep.tile([P, PACK], F32, name="gain")
         nc.sync.dma_start(gain[:], gn.rearrange("(p t) o -> p (t o)", t=PACK))
         n1_sb = keep.tile([P, S // 16], U16, name="n1_sb")
@@ -58,21 +61,30 @@ def tile_picked_hashprod_none_p_kernel(tc, x_words, x_scales, w1, gn, w2, offs, 
         for b in range(1, 4):
             nc.sync.dma_start(x_plane[b:P:32, :].bitcast(I32), picked_bytes[8 * b : P : 32, :].bitcast(I32))
 
+        x_codes = keep.tile([P, S], U32, name="x_codes", align_bytes=64)
+        nc.vector.tensor_copy(x_codes[:], word_table[:].indirect(offs_sb[:]))
+
+        early = W1_EARLY // PACK
         w1_grouped = keep.tile([P, PACK * H], BF16, name="w1_grouped", align_bytes=64)
         w1_dst = w1_grouped[:].rearrange("p (t m j) -> p m t j", t=PACK, j=PACK)
-        w1_src = w1_raw[:].rearrange("p (j m t) -> p m t j", j=PACK, t=PACK)
-        nc.vector.tensor_copy(w1_dst[:, :W1_SPLIT], w1_src[:, :W1_SPLIT])
-        nc.scalar.copy(w1_dst[:, W1_SPLIT:], w1_src[:, W1_SPLIT:])
+        nc.vector.tensor_copy(w1_dst[:, :early], w1_early[:].rearrange("p (j m t) -> p m t j", j=PACK, t=PACK))
+        late_src = w1_late[:].rearrange("p (j m t) -> p m t j", j=PACK, t=PACK)
         w1_codes = keep.tile([P, H], U32, name="w1_codes", align_bytes=64)
         w1_plane = keep.tile([P, H], U8, name="w1_plane", align_bytes=64)
-        nc.vector.quantize_mx(out=w1_codes[:].bitcast(FP8X4), scales=w1_plane[:], in_=w1_grouped[:])
+        for t in range(PACK):
+            if t % 2 == 0:
+                nc.vector.tensor_copy(w1_dst[:, early:, t, :], late_src[:, :, t, :])
+            else:
+                nc.scalar.copy(w1_dst[:, early:, t, :], late_src[:, :, t, :])
+            rows = slice(t * P, (t + 1) * P)
+            nc.vector.quantize_mx(
+                out=w1_codes[:, rows].bitcast(FP8X4),
+                scales=w1_plane[:, rows],
+                in_=w1_grouped[:, t * PACK * P : (t + 1) * PACK * P],
+            )
 
         w2_raw = keep.tile([P, PACK * N], F32, name="w2_raw", tag="raw")
         nc.sync.dma_start(w2_raw[:], w2.rearrange("(p j) c -> p (j c)", j=PACK))
-
-        x_codes = keep.tile([P, S], U32, name="x_codes", align_bytes=64)
-        for c0 in range(0, S, HALF):
-            nc.vector.tensor_copy(x_codes[:, c0 : c0 + HALF], word_table[:].indirect(entries(offs_sb, c0, HALF)))
 
         y = [keep.tile([P, 2 * S], F32, name=f"y{t}") for t in range(PACK)]
         gained = [keep.tile([P, 2 * S], F32, name=f"gained{t}") for t in range(PACK)]

from contextlib import ExitStack

import concourse.mybir as mybir

K, T, S, N, H = 512, 2048, 512, 512, 512
FLOPS = 2 * K * H * S + 2 * H * N * S

F32 = mybir.dt.float32
BF16 = mybir.dt.bfloat16
I32 = mybir.dt.int32
U32 = mybir.dt.uint32
U16 = mybir.dt.uint16
U8 = mybir.dt.uint8
FP8X4 = mybir.dt.float8_e4m3fn_x4
MULT = mybir.AluOpType.mult
SUB = mybir.AluOpType.subtract
COPY = mybir.ActivationFunctionType.Copy

P = 128
PACK = 4
HALF = S // 2
W1_EARLY = 256
CHUNKS = ((0, 256), (256, 128), (384, 128))


def entries(lists, start, count):
    return lists[:, start // 16 : (start + count) // 16]


def tile_picked_hashprod_none_p_kernel(tc, x_words, x_scales, w1, gn, w2, offs, n1, n2, out):
    nc = tc.nc
    with ExitStack() as ctx:
        keep = ctx.enter_context(tc.tile_pool(name="keep", bufs=1))
        psum = ctx.enter_context(tc.psum_pool(name="psum", bufs=8))

        offs_sb = keep.tile([P, S // 16], U16, name="offs_sb")
        nc.sync.dma_start(offs_sb[:], offs)
        scale_table = keep.tile([P, T], U8, name="scale_table")
        nc.sync.dma_start(
            scale_table[:].bitcast(I32),
            x_scales[0].bitcast(I32).unsqueeze(1).broadcast_to([16, 8, T // 4]),
        )
        word_table = keep.tile([P, T], U32, name="word_table")
        nc.sync.dma_start(word_table[:].bitcast(I32), x_words[0].rearrange("p c r -> p (c r)").bitcast(I32))
        w1_rows = w1.rearrange("(p j) c -> p j c", j=PACK)
        w1_early = keep.tile([P, PACK * W1_EARLY], F32, name="w1_early", tag="raw")
        nc.sync.dma_start(w1_early[:].rearrange("p (j c) -> p j c", j=PACK), w1_rows[:, :, :W1_EARLY])
        w1_late = keep.tile([P, PACK * (H - W1_EARLY)], F32, name="w1_late")
        nc.sync.dma_start(w1_late[:].rearrange("p (j c) -> p j c", j=PACK), w1_rows[:, :, W1_EARLY:])
        gain = keep.tile([P, PACK], F32, name="gain")
        nc.sync.dma_start(gain[:], gn.rearrange("(p t) o -> p (t o)", t=PACK))
        n1_sb = keep.tile([P, S // 16], U16, name="n1_sb")
        nc.sync.dma_start(n1_sb[:], n1)
        n2_sb = keep.tile([P, S // 16], U16, name="n2_sb")
        nc.sync.dma_start(n2_sb[:], n2)

        picked_bytes = keep.tile([P, S], U8, name="picked_bytes", align_bytes=64)
        nc.vector.tensor_copy(picked_bytes[:], scale_table[:].indirect(offs_sb[:]))
        x_plane = keep.tile([P, S], U8, name="x_plane", align_bytes=64)
        nc.vector.tensor_copy(x_plane[:].bitcast(I32), picked_bytes[:].bitcast(I32))
        for b in range(1, 4):
            nc.sync.dma_start(x_plane[b:P:32, :].bitcast(I32), picked_bytes[8 * b : P : 32, :].bitcast(I32))

        x_codes = keep.tile([P, S], U32, name="x_codes", align_bytes=64)
        nc.vector.tensor_copy(x_codes[:], word_table[:].indirect(offs_sb[:]))

        early = W1_EARLY // PACK
        w1_grouped = keep.tile([P, PACK * H], BF16, name="w1_grouped", align_bytes=64)
        w1_dst = w1_grouped[:].rearrange("p (t m j) -> p m t j", t=PACK, j=PACK)
        nc.vector.tensor_copy(w1_dst[:, :early], w1_early[:].rearrange("p (j m t) -> p m t j", j=PACK, t=PACK))
        late_src = w1_late[:].rearrange("p (j m t) -> p m t j", j=PACK, t=PACK)
        w1_codes = keep.tile([P, H], U32, name="w1_codes", align_bytes=64)
        w1_plane = keep.tile([P, H], U8, name="w1_plane", align_bytes=64)
        for t in range(PACK):
            if t % 2 == 0:
                nc.vector.tensor_copy(w1_dst[:, early:, t, :], late_src[:, :, t, :])
            else:
                nc.scalar.copy(w1_dst[:, early:, t, :], late_src[:, :, t, :])
            rows = slice(t * P, (t + 1) * P)
            nc.vector.quantize_mx(
                out=w1_codes[:, rows].bitcast(FP8X4),
                scales=w1_plane[:, rows],
                in_=w1_grouped[:, t * PACK * P : (t + 1) * PACK * P],
            )

        w2_raw = keep.tile([P, PACK * N], F32, name="w2_raw", tag="raw")
        nc.sync.dma_start(w2_raw[:], w2.rearrange("(p j) c -> p (j c)", j=PACK))

        y = [keep.tile([P, 2 * S], F32, name=f"y{t}") for t in range(PACK)]
        gained = [keep.tile([P, 2 * S], F32, name=f"gained{t}") for t in range(PACK)]
        banks = []
        for t in range(PACK):
            rows = slice(t * P, (t + 1) * P)
            width = HALF if t == 0 else S
            parts = []
            for c0 in range(0, S, width):
                cols = slice(c0, c0 + width)
                bank = psum.tile([P, S], F32, name="bank")
                nc.tensor.matmul_mx(
                    out=bank[:, :width],
                    lhsT=w1_codes[:, rows].bitcast(FP8X4),
                    lhsT_scale=w1_plane[:, rows],
                    rhs=x_codes[:, cols].bitcast(FP8X4),
                    rhs_scale=x_plane[:, cols],
                    start=True,
                    stop=True,
                )
                nc.scalar.copy(y[t][:, cols], bank[:, :width])
                parts.append((cols, bank[:, :width]))
            banks.append(parts)
            if t > 0:
                for cols, part in banks[t - 1]:
                    nc.scalar.activation(gained[t - 1][:, cols], part, COPY, scale=gain[:, t - 1 : t])
        for cols, part in banks[PACK - 1]:
            nc.scalar.activation(gained[PACK - 1][:, cols], part, COPY, scale=gain[:, PACK - 1 : PACK])

        w2_grouped = keep.tile([P, PACK * N], BF16, name="w2_grouped", align_bytes=64)
        w2_dst = w2_grouped[:].rearrange("p (c i j) -> p c j i", i=4, j=PACK)
        w2_src = w2_raw[:].rearrange("p (j c i) -> p c j i", i=4, j=PACK)
        w2_codes = keep.tile([P, N], U32, name="w2_codes", align_bytes=64)
        w2_plane = keep.tile([P, N], U8, name="w2_plane", align_bytes=64)

        firsts = [keep.tile([P, S], F32, name=f"first{t}") for t in range(PACK)]
        scaled = [keep.tile([P, S], F32, name=f"scaled{t}") for t in range(PACK)]
        halved = [keep.tile([P, S], F32, name=f"halved{t}") for t in range(PACK)]
        nc.vector.tensor_copy(firsts[0][:], y[0][:].indirect(n1_sb[:]))
        for t in range(PACK):
            if t + 1 < PACK:
                nc.vector.tensor_copy(firsts[t + 1][:], y[t + 1][:].indirect(n1_sb[:]))
            nc.vector.tensor_tensor(scaled[t][:], gained[t][:].indirect(n2_sb[:]), firsts[t][:], MULT)
            nc.scalar.copy(w2_dst[:, 32 * t : 32 * (t + 1)], w2_src[:, 32 * t : 32 * (t + 1)])
            nc.scalar.mul(halved[t][:], scaled[t][:], 0.5)
        nc.vector.quantize_mx(out=w2_codes[:].bitcast(FP8X4), scales=w2_plane[:], in_=w2_grouped[:])

        out_rows = out.rearrange("(t p) j -> p t j", p=P)

        def gather_chunk(c0, n):
            z = keep.tile([P, PACK * n], F32, name=f"z{c0}", tag="turn_a" if c0 + n == S else f"z{c0}", align_bytes=64)
            for t in range(PACK):
                nc.vector.tensor_tensor(
                    z[:, t * n : (t + 1) * n], scaled[t][:].indirect(entries(n1_sb, c0, n)), halved[t][:, c0 : c0 + n], SUB
                )
            return z

        def group_chunk(c0, n, z):
            grouped = keep.tile([P, PACK * n], BF16, name=f"z_grouped{c0}", tag="turn_a" if c0 == 0 else "turn_b", align_bytes=64)
            dst = grouped[:].rearrange("p (c i t) -> p c t i", i=4, t=PACK)
            src = z[:].rearrange("p (t c i) -> p c t i", i=4, t=PACK)
            if c0 + n == S:
                nc.vector.tensor_copy(dst, src)
            else:
                nc.scalar.copy(dst, src)
            return grouped

        def finish_chunk(c0, n, grouped):
            codes = keep.tile([P, n], U32, name=f"z_codes{c0}", align_bytes=64)
            plane = keep.tile([P, n], U8, name=f"z_plane{c0}", align_bytes=64)
            nc.vector.quantize_mx(out=codes[:].bitcast(FP8X4), scales=plane[:], in_=grouped[:])
            for pair in range(2):
                bank = psum.tile([P, S], F32, name="bank")
                for u in range(2):
                    rows = slice((2 * pair + u) * P, (2 * pair + u + 1) * P)
                    nc.tensor.matmul_mx(
                        out=bank[:, u * n : (u + 1) * n],
                        lhsT=w2_codes[:, rows].bitcast(FP8X4),
                        lhsT_scale=w2_plane[:, rows],
                        rhs=codes[:].bitcast(FP8X4),
                        rhs_scale=plane[:],
                        start=True,
                        stop=True,
                    )
                result = keep.tile([P, 2 * n], F32, name=f"result{c0}_{pair}")
                if c0 + n == S and pair == 1:
                    nc.vector.tensor_copy(result[:], bank[:, : 2 * n])
                else:
                    nc.scalar.copy(result[:], bank[:, : 2 * n])
                queue = nc.scalar if c0 + n == S and pair == 0 else nc.sync
                queue.dma_start(
                    out_rows[:, 2 * pair : 2 * pair + 2, c0 : c0 + n], result[:].rearrange("p (u j) -> p u j", u=2)
                )

        first_chunk, second_chunk, last_chunk = CHUNKS
        grouped_first = group_chunk(*first_chunk, gather_chunk(*first_chunk))
        grouped_second = group_chunk(*second_chunk, gather_chunk(*second_chunk))
        finish_chunk(*first_chunk, grouped_first)
        z_last = gather_chunk(*last_chunk)
        finish_chunk(*second_chunk, grouped_second)
        finish_chunk(*last_chunk, group_chunk(*last_chunk, z_last))
